import numpy as np
import ml_dtypes


def mxq(x, axis, fmt="e4m3"):
    dtype, down = {"e4m3": (ml_dtypes.float8_e4m3fn, 7), "e5m2": (ml_dtypes.float8_e5m2, 14)}[fmt]
    v = np.moveaxis(np.asarray(x, np.float32).astype(ml_dtypes.bfloat16).astype(np.float64), axis, -1)
    blocks = v.reshape(v.shape[:-1] + (-1, 32))
    amax = np.abs(blocks).max(-1, keepdims=True)
    byte = np.maximum(np.where(amax > 0, np.frexp(amax)[1] - 1 + 127, 0) - down, 1)
    scale = np.exp2(byte - 127.0)
    codes = (blocks / scale).astype(np.float32).astype(dtype).astype(np.float64)
    return np.moveaxis((codes * scale).reshape(v.shape), -1, axis)


WIDE = False


def mx_kscale(k):
    if not WIDE:
        return np.ones(k)
    levels = np.array([10, -10, 5, -5, 0])
    if k % 512:
        return np.exp2(np.random.permutation(np.resize(levels, k // 32))).repeat(32)
    a = np.empty((k // 512, 16))
    for p in range(k // 512):
        a[p, :8] = np.random.permutation(np.resize(levels, 8))
        for g in range(8):
            far = levels[np.abs(levels - a[p, g]) >= 10]
            a[p, g + 8] = far[np.random.randint(len(far))]
    return np.exp2(a.ravel()).repeat(32)


def f64(x):
    return np.asarray(x).astype(np.float64)


def striped(idx):
    return np.tile(idx.reshape(-1, 16).T, (8, 1)).astype(np.uint16)


def unstriped(offs):
    return offs[:16].T.reshape(-1).astype(np.int64)


def striped8(idx):
    return np.concatenate([x.reshape(-1, 16).T for x in idx]).astype(np.uint16)


def runs(offs, k):
    lists = np.stack([offs[16 * r : 16 * r + 16].T.reshape(-1) for r in range(8)]).astype(np.int64)
    return lists[np.arange(k) % 512 // 64]


def pack_weight(w):
    k, n = w.shape
    w = f64(np.asarray(w, np.float32).astype(ml_dtypes.bfloat16)).reshape(k // 32, 32, n)
    amax = np.abs(w).max(1)
    byte = np.clip(np.where(amax > 0, np.frexp(amax)[1] - 1 + 127 - 7, 1), 1, 254)
    scaled = (w * np.exp2(127.0 - byte)[:, None, :]).reshape(k, n).astype(np.float32)
    words = np.ascontiguousarray(scaled.reshape(k // 512, 128, 4, n).transpose(0, 1, 3, 2)).astype(ml_dtypes.float8_e4m3fn).view(np.uint8)
    return words, np.ascontiguousarray(byte.astype(np.uint8).reshape(k // 512, 16, n))


def unpack_weight(words, scales):
    g, p, n, _ = words.shape
    vals = np.ascontiguousarray(words).view(ml_dtypes.float8_e4m3fn).astype(np.float64) * np.repeat(np.exp2(scales.astype(np.float64) - 127.0), 8, axis=1)[..., None]
    return vals.transpose(0, 1, 3, 2).reshape(g * 512, n)


E2M1 = np.array([0.0, 0.5, 1.0, 1.5, 2.0, 3.0, 4.0, 6.0, -0.0, -0.5, -1.0, -1.5, -2.0, -3.0, -4.0, -6.0])


def pack_fp4(w):
    k, n = w.shape
    w = f64(np.asarray(w, np.float32).astype(ml_dtypes.bfloat16)).reshape(k // 32, 32, n)
    amax = np.abs(w).max(1)
    mant, ex = np.frexp(amax / 6.0)
    byte = np.clip(np.where(amax > 0, np.where(mant > 0.5, ex, ex - 1) + 127, 1), 1, 254)
    scaled = (w * np.exp2(127.0 - byte)[:, None, :]).reshape(k, n).astype(np.float32)
    c = np.ascontiguousarray(scaled.reshape(k // 512, 128, 4, n).transpose(0, 1, 3, 2)).astype(ml_dtypes.float4_e2m1fn).view(np.uint8) & 0xF
    words = (c[..., 0::2] | (c[..., 1::2] << 4)).reshape(k // 512, 128, 2 * n)
    return np.ascontiguousarray(words), np.ascontiguousarray(byte.astype(np.uint8).reshape(k // 512, 16, n))


def unpack_fp4(words, scales):
    g, _, n = scales.shape
    words = np.ascontiguousarray(words).reshape(g, 128, n, 2)
    nib = np.empty((g, 128, n, 4), np.uint8)
    nib[..., 0::2] = words & 0xF
    nib[..., 1::2] = words >> 4
    vals = E2M1[nib] * np.repeat(np.exp2(scales.astype(np.float64) - 127.0), 8, axis=1)[..., None]
    return vals.transpose(0, 1, 3, 2).reshape(g * 512, n)


def planes(y):
    n, m = y.shape
    v = y.astype(np.float32).astype(ml_dtypes.bfloat16).astype(np.float64).reshape(n // 32, 32, m)
    top = np.abs(v).max(1)
    byte = np.clip(np.where(top > 0, np.frexp(top)[1] - 1 + 127 - 7, 1), 1, 254)
    codes = (v * np.exp2(127.0 - byte)[:, None, :]).reshape(n, m).astype(np.float32).astype(ml_dtypes.float8_e4m3fn).view(np.uint8)
    words = codes.reshape(n // 512, 128, 4, m).transpose(0, 1, 3, 2)
    return np.ascontiguousarray(words), np.ascontiguousarray(byte.astype(np.uint8).reshape(n // 512, 16, m))


K, T, S, V, N, G, H = 512, 2048, 512, 256, 512, 2048, 512


def setup_inputs():
    n = np.random.standard_normal
    s = mx_kscale(K)[:, None]
    u = mx_kscale(H)
    packed_xT = pack_weight(n((K, T)) * s)
    packed_dT = pack_weight(n((K, G)) / s)
    packed_w1 = pack_fp4(n((H, N)) / np.sqrt(H) / u[:, None])
    return {
        "x_words": packed_xT[0],
        "x_scales": packed_xT[1],
        "d_words": packed_dT[0],
        "d_scales": packed_dT[1],
        "gn": (np.random.uniform(0.5, 1.5, (H, 1)) * u[:, None]).astype(np.float32),
        "w1_words": packed_w1[0],
        "w1_scales": packed_w1[1],
        "offs": striped(np.random.permutation(T)[:S]),
        "kidx": striped8(np.random.randint(0, G, (8, H))),
        "l1": striped8(np.stack([np.random.permutation(S)[:V] for _ in range(8)])),
        "l2": striped8(np.stack([np.random.permutation(S)[:V] for _ in range(8)])),
    }


def reference(x_words, x_scales, d_words, d_scales, gn, w1_words, w1_scales, offs, kidx, l1, l2):
    d_kidx = unpack_weight(d_words, d_scales)[np.arange(K)[:, None], runs(kidx, K)]
    xq = unpack_weight(x_words, x_scales)[:, unstriped(offs)]
    s = 0.0625 * (d_kidx.T @ xq)
    z = f64(gn) * (np.abs(s[np.arange(H)[:, None], runs(l1, H)] - (s[np.arange(H)[:, None], runs(l2, H)])))
    out_0 = unpack_fp4(w1_words, w1_scales).T @ mxq(z, 0, "e4m3")
    return (out_0,) + planes(out_0)

@@ -1,0 +1,219 @@
+from contextlib import ExitStack
+
+import concourse.mybir as mybir
+
+K, T, S, V, N, G, H = 512, 2048, 512, 256, 512, 2048, 512
+FLOPS = 2 * K * H * S + 2 * H * N * V
+
+F32 = mybir.dt.float32
+BF16 = mybir.dt.bfloat16
+I32 = mybir.dt.int32
+U32 = mybir.dt.uint32
+U16 = mybir.dt.uint16
+U8 = mybir.dt.uint8
+FP8X4 = mybir.dt.float8_e4m3fn_x4
+FP4X4 = mybir.dt.float4_e2m1fn_x4
+ACT = mybir.ActivationFunctionType
+ALU = mybir.AluOpType
+
+P = 128
+PACK = 4
+HALF = V // 2
+
+
+def tile_picked_scorepair_none_po_kernel(
+    tc, x_words, x_scales, d_words, d_scales, gn, w1_words, w1_scales, offs, kidx, l1, l2, out_0, out_1, out_2
+):
+    nc = tc.nc
+    with ExitStack() as ctx:
+        sb = ctx.enter_context(tc.tile_pool(name="sb", bufs=1))
+        ps = ctx.enter_context(tc.psum_pool(name="ps", bufs=1))
+
+        shared = ctx.enter_context(tc.tile_pool(name="shared", bufs=1))
+
+        def tile(name, shape, dtype):
+            return sb.tile(shape, dtype, name=name, align_bytes=64)
+
+        def tile_at(offset, name, shape, dtype):
+            return shared.tile(shape, dtype, name=name, align_bytes=64, offset=offset)
+
+        kidx_t = tile("kidx_t", [P, H // 16], U16)
+        offs_t = tile("offs_t", [P, S // 16], U16)
+        l1_t = tile("l1_t", [P, V // 16], U16)
+        l2_t = tile("l2_t", [P, V // 16], U16)
+        ds_win = tile_at(0, "ds_win", [P, G], U8)
+        xs_win = tile_at(G, "xs_win", [P, T], U8)
+        dw_win = tile_at(G + 5 * T, "dw_win", [P, G], U32)
+        xw_win = tile_at(G + T, "xw_win", [P, T], U32)
+        warm_in = tile("warm_in", [P, 1], F32)
+        warm_out = tile("warm_out", [P, 1], F32)
+
+        nc.vector.memset(ds_win[:].bitcast(I32), 0)
+        nc.vector.memset(xs_win[:].bitcast(I32), 0)
+
+        nc.sync.dma_start(kidx_t[:], kidx)
+        nc.sync.dma_start(offs_t[:], offs)
+        nc.sync.dma_start(l1_t[:], l1)
+        nc.sync.dma_start(l2_t[:], l2)
+        nc.sync.dma_start(out=ds_win[0:P:8, :].bitcast(I32), in_=d_scales[0].bitcast(I32))
+        nc.sync.dma_start(out=xs_win[0:P:8, :].bitcast(I32), in_=x_scales[0].bitcast(I32))
+        nc.sync.dma_start(out=dw_win[:].bitcast(I32), in_=d_words[0].rearrange("p n t -> p (n t)").bitcast(I32))
+        nc.sync.dma_start(out=xw_win[:].bitcast(I32), in_=x_words[0].rearrange("p n t -> p (n t)").bitcast(I32))
+
+        planes = tile("planes", [P, H + S], U8)
+        nc.vector.memset(planes[:].bitcast(I32), 0)
+        nc.vector.memset(warm_in[:], 0.0)
+        nc.scalar.activation(out=warm_out[:], in_=warm_in[:], func=ACT.Abs)
+
+        picked_bytes = tile("picked_bytes", [P, H + S], U8)
+        nc.vector.tensor_copy(picked_bytes[:, 0:H], ds_win[:].indirect(kidx_t[:]))
+        nc.vector.tensor_copy(picked_bytes[:, H : H + S], xs_win[:].indirect(offs_t[:]))
+        for j in range(4):
+            nc.scalar.dma_start(out=planes[j:P:32, :].bitcast(I32), in_=picked_bytes[8 * j : P : 32, :].bitcast(I32))
+
+        dw_picked = tile_at(G + 9 * T, "dw_picked", [P, H], U32)
+        nc.vector.tensor_copy(dw_picked[:], dw_win[:].indirect(kidx_t[:]))
+        w1w_raw = tile_at(G + 5 * T, "w1w_raw", [P, 2 * N], U8)
+        nc.sync.dma_start(out=w1w_raw[:].bitcast(I32), in_=w1_words[0].bitcast(I32))
+        dw_dealt = tile("dw_dealt", [P, H], U32)
+        nc.vector.tensor_copy(
+            out=dw_dealt[:].rearrange("p (t m) -> p m t", t=PACK), in_=dw_picked[:].rearrange("p (m t) -> p m t", t=PACK)
+        )
+        xw_picked = [tile_at(G + 9 * T + 1024 * h, "xw_picked%d" % h, [P, S // 2], U32) for h in range(2)]
+        nc.vector.tensor_copy(xw_picked[0][:], xw_win[:].indirect(offs_t[:, 0:16]))
+        ds_dealt = tile("ds_dealt", [P, H], U8)
+        nc.vector.tensor_copy(
+            out=ds_dealt[:].rearrange("p (t m) -> p m t", t=PACK), in_=planes[:, 0:H].rearrange("p (m t) -> p m t", t=PACK)
+        )
+        nc.vector.tensor_copy(xw_picked[1][:], xw_win[:].indirect(offs_t[:, 16:32]))
+
+        w1w = tile_at(G + T, "w1w", [P, 2 * N], U8)
+        nc.vector.tensor_copy(
+            out=w1w[:].rearrange("p (t m b) -> p m t b", t=PACK, b=2),
+            in_=w1w_raw[:].rearrange("p (m t b) -> p m t b", t=PACK, b=2),
+        )
+        gn_t = tile_at(G + T + 2 * N, "gn_t", [P, PACK], F32)
+        w1s_raw = tile_at(G + T + 3 * N, "w1s_raw", [P, N], U8)
+        nc.sync.dma_start(out=gn_t[:], in_=gn.rearrange("(p t) o -> p (t o)", t=PACK))
+        nc.vector.memset(w1s_raw[:].bitcast(I32), 0)
+        for q in range(4):
+            nc.sync.dma_start(
+                out=w1s_raw[32 * q : 32 * q + 4, :].bitcast(I32), in_=w1_scales[0, 4 * q : 4 * q + 4, :].bitcast(I32)
+            )
+
+        scores = [tile_at(G + 10 * T + 4 * S * t, "scores%d" % t, [P, S], F32) for t in range(PACK)]
+
+        def score_pass(dst, t, h):
+            nc.tensor.matmul_mx(
+                out=dst,
+                lhsT=dw_dealt[:, P * t : P * (t + 1)].bitcast(FP8X4),
+                lhsT_scale=ds_dealt[:, P * t : P * (t + 1)],
+                rhs=xw_picked[h][:].bitcast(FP8X4),
+                rhs_scale=planes[:, H + 256 * h : H + 256 * (h + 1)],
+                start=True,
+                stop=True,
+            )
+
+        lead = [ps.tile([P, S // 2], F32, name="lead_bank%d" % h) for h in range(2)]
+        banks = [ps.tile([P, S], F32, name="score_bank%d" % t) for t in range(1, PACK)]
+        for h in range(2):
+            cols = slice(256 * h, 256 * (h + 1))
+            score_pass(lead[h][:], 0, h)
+            nc.scalar.copy(out=scores[0][:, cols], in_=lead[h][:])
+            for t in range(1, PACK):
+                score_pass(banks[t - 1][:, cols], t, h)
+        for t in range(1, PACK):
+            nc.scalar.copy(out=scores[t][:], in_=banks[t - 1][:])
+
+        first = tile("first", [P, PACK, V], F32)
+        diff = tile("diff", [P, PACK, V], F32)
+        size = tile("size", [P, PACK, V], F32)
+        z32 = tile("z32", [P, PACK, HALF], F32)
+
+        def fetch_first(t, lo, hi):
+            nc.vector.tensor_copy(first[:, t, lo:hi], scores[t][:].indirect(l1_t[:, lo // 16 : hi // 16]))
+
+        def fetch_second(t, lo, hi):
+            nc.vector.tensor_tensor(
+                diff[:, t, lo:hi], scores[t][:].indirect(l2_t[:, lo // 16 : hi // 16]), first[:, t, lo:hi], ALU.subtract
+            )
+            nc.scalar.activation(out=size[:, t, lo:hi], in_=diff[:, t, lo:hi], func=ACT.Abs, scale=0.0625)
+            if lo == 0:
+                nc.scalar.activation(out=z32[:, t, :], in_=size[:, t, 0:HALF], func=ACT.Copy, scale=gn_t[:, t : t + 1])
+
+        z_codes = tile("z_codes", [P, V], U32)
+        z_scales = tile("z_scales", [P, V], U8)
+        y_codes = tile("y_codes", [P, V], U32)
+        y_scales = tile("y_scales", [P, V], U8)
+        z16 = [tile("z16_%d" % h, [P, HALF, PACK], BF16) for h in range(2)]
+        y16 = [tile("y16_%d" % h, [P, HALF, PACK], BF16) for h in range(2)]
+        y32 = [tile("y32_%d" % h, [P, PACK, HALF], F32) for h in range(2)]
+        out_rows = out_0.rearrange("(p t) v -> p t v", t=PACK)
+        halves = [slice(0, HALF), slice(HALF, V)]
+
+        def quantize(codes, scales, src, h):
+            nc.vector.quantize_mx(
+                out=codes[:, halves[h]].bitcast(FP8X4), scales=scales[:, halves[h]], in_=src[:].rearrange("p v t -> p (v t)")
+            )
+
+        def value_pass(dst, t, h):
+            nc.tensor.matmul_mx(
+                out=dst,
+                lhsT=w1w[:, 2 * P * t : 2 * P * (t + 1)].bitcast(FP4X4),
+                lhsT_scale=w1s[:, P * t : P * (t + 1)],
+                rhs=z_codes[:, halves[h]].bitcast(FP8X4),
+                rhs_scale=z_scales[:, halves[h]],
+                start=True,
+                stop=True,
+            )
+
+        fetch_first(0, 0, V)
+        fetch_second(0, 0, V)
+        fetch_first(1, 0, V)
+        w1s = tile_at(G + 10 * T, "w1s", [P, N], U8)
+        nc.vector.tensor_copy(
+            out=w1s[:].rearrange("p (t m) -> p m t", t=PACK), in_=w1s_raw[:].rearrange("p (m t) -> p m t", t=PACK)
+        )
+        fetch_first(2, 0, HALF)
+        fetch_second(1, 0, V)
+        fetch_first(3, 0, HALF)
+        fetch_second(2, 0, HALF)
+        fetch_second(3, 0, HALF)
+        nc.scalar.copy(out=z16[0][:], in_=z32[:].rearrange("p t v -> p v t"))
+        fetch_first(2, HALF, V)
+        fetch_first(3, HALF, V)
+        fetch_second(2, HALF, V)
+        fetch_second(3, HALF, V)
+
+        quantize(z_codes, z_scales, z16[0], 0)
+        bank0 = ps.tile([P, PACK, HALF], F32, name="value_bank0")
+        for t in range(PACK):
+            value_pass(bank0[:, t, :], t, 0)
+        nc.vector.tensor_tensor(
+            out=z16[1][:],
+            in0=size[:, :, halves[1]].rearrange("p t v -> p v t"),
+            in1=gn_t[:].unsqueeze(1).to_broadcast([P, HALF, PACK]),
+            op=ALU.mult,
+        )
+        quantize(z_codes, z_scales, z16[1], 1)
+        nc.scalar.copy(out=y16[0][:], in_=bank0[:].rearrange("p t v -> p v t"))
+        nc.scalar.copy(out=y32[0][:], in_=bank0[:])
+        nc.sync.dma_start(out=out_rows[:, :, halves[0]], in_=y32[0][:])
+        quantize(y_codes, y_scales, y16[0], 0)
+
+        for pair in range(2):
+            rows = slice(2 * pair, 2 * pair + 2)
+            bank = ps.tile([P, 2, HALF], F32, name="value_bank1_%d" % pair)
+            for u in range(2):
+                value_pass(bank[:, u, :], 2 * pair + u, 1)
+            nc.vector.tensor_copy(out=y16[1][:, :, rows], in_=bank[:].rearrange("p t v -> p v t"))
+            nc.scalar.copy(out=y32[1][:, rows, :], in_=bank[:])
+            queue = nc.sync if pair == 0 else nc.scalar
+            queue.dma_start(out=out_rows[:, rows, halves[1]], in_=y32[1][:, rows, :])
+        quantize(y_codes, y_scales, y16[1], 1)
+        nc.sync.dma_start(out=out_1[0].rearrange("p v r -> p (v r)").bitcast(I32), in_=y_codes[:].bitcast(I32))
+        for q in range(4):
+            queue = nc.sync if q < 2 else nc.scalar
+            queue.dma_start(
+                out=out_2[0, 4 * q : 4 * q + 4, :].bitcast(I32), in_=y_scales[32 * q : 32 * q + 4, :].bitcast(I32)
+            )

@@ -69,61 +69,58 @@ def tile_picked_scorepair_none_po_kernel(
         nc.vector.tensor_copy(picked_bytes[:, 0:H], ds_win[:].indirect(kidx_t[:]))
         nc.vector.tensor_copy(picked_bytes[:, H : H + S], xs_win[:].indirect(offs_t[:]))
         for j in range(4):
-            nc.scalar.dma_start(out=planes[j:P:32, :].bitcast(I32), in_=picked_bytes[8 * j : P : 32, :].bitcast(I32))
+            nc.sync.dma_start(out=planes[j:P:32, :].bitcast(I32), in_=picked_bytes[8 * j : P : 32, :].bitcast(I32))
 
         dw_picked = tile_at(G + 9 * T, "dw_picked", [P, H], U32)
         nc.vector.tensor_copy(dw_picked[:], dw_win[:].indirect(kidx_t[:]))
-        w1w_raw = tile_at(G + 5 * T, "w1w_raw", [P, 2 * N], U8)
+        gn_t = tile_at(G + 5 * T, "gn_t", [P, PACK], F32)
+        w1w_raw = tile_at(G + 5 * T + N, "w1w_raw", [P, 2 * N], U8)
         nc.sync.dma_start(out=w1w_raw[:].bitcast(I32), in_=w1_words[0].bitcast(I32))
-        dw_dealt = tile("dw_dealt", [P, H], U32)
-        nc.vector.tensor_copy(
-            out=dw_dealt[:].rearrange("p (t m) -> p m t", t=PACK), in_=dw_picked[:].rearrange("p (m t) -> p m t", t=PACK)
-        )
-        xw_picked = [tile_at(G + 9 * T + 1024 * h, "xw_picked%d" % h, [P, S // 2], U32) for h in range(2)]
-        nc.vector.tensor_copy(xw_picked[0][:], xw_win[:].indirect(offs_t[:, 0:16]))
-        ds_dealt = tile("ds_dealt", [P, H], U8)
-        nc.vector.tensor_copy(
-            out=ds_dealt[:].rearrange("p (t m) -> p m t", t=PACK), in_=planes[:, 0:H].rearrange("p (m t) -> p m t", t=PACK)
-        )
-        nc.vector.tensor_copy(xw_picked[1][:], xw_win[:].indirect(offs_t[:, 16:32]))
-
-        w1w = tile_at(G + T, "w1w", [P, 2 * N], U8)
-        nc.vector.tensor_copy(
-            out=w1w[:].rearrange("p (t m b) -> p m t b", t=PACK, b=2),
-            in_=w1w_raw[:].rearrange("p (m t b) -> p m t b", t=PACK, b=2),
-        )
-        gn_t = tile_at(G + T + 2 * N, "gn_t", [P, PACK], F32)
-        w1s_raw = tile_at(G + T + 3 * N, "w1s_raw", [P, N], U8)
         nc.sync.dma_start(out=gn_t[:], in_=gn.rearrange("(p t) o -> p (t o)", t=PACK))
+
+        def deal(dst, src, run, width):
+            nc.vector.tensor_copy(
+                out=dst.rearrange("p (t c i b) -> p c t i b", t=PACK, i=run, b=width),
+                in_=src.rearrange("p (c i t b) -> p c t i b", t=PACK, i=run, b=width),
+            )
+
+        dw_dealt = tile("dw_dealt", [P, H], U32)
+        deal(dw_dealt[:], dw_picked[:], 4, 1)
+        xw_picked = tile_at(G + 9 * T, "xw_picked", [P, S], U32)
+        nc.vector.tensor_copy(xw_picked[:, 0:256], xw_win[:].indirect(offs_t[:, 0:16]))
+        ds_dealt = tile("ds_dealt", [P, H], U8)
+        deal(ds_dealt[:], planes[:, 0:H], 16, 1)
+        nc.vector.tensor_copy(xw_picked[:, 256:512], xw_win[:].indirect(offs_t[:, 16:32]))
+
+        w1s_raw = tile_at(G + T + 2 * N, "w1s_raw", [P, N], U8)
         nc.vector.memset(w1s_raw[:].bitcast(I32), 0)
         for q in range(4):
             nc.sync.dma_start(
                 out=w1s_raw[32 * q : 32 * q + 4, :].bitcast(I32), in_=w1_scales[0, 4 * q : 4 * q + 4, :].bitcast(I32)
             )
 
+        w1w = tile_at(G + T, "w1w", [P, 2 * N], U8)
+        deal(w1w[:], w1w_raw[:], 8, 2)
+
         scores = [tile_at(G + 10 * T + 4 * S * t, "scores%d" % t, [P, S], F32) for t in range(PACK)]
 
-        def score_pass(dst, t, h):
+        def score(t, lo, hi):
+            bank = ps.tile([P, hi - lo], F32, name="score_bank%d_%d" % (t, lo))
             nc.tensor.matmul_mx(
-                out=dst,
+                out=bank[:],
                 lhsT=dw_dealt[:, P * t : P * (t + 1)].bitcast(FP8X4),
                 lhsT_scale=ds_dealt[:, P * t : P * (t + 1)],
-                rhs=xw_picked[h][:].bitcast(FP8X4),
-                rhs_scale=planes[:, H + 256 * h : H + 256 * (h + 1)],
+                rhs=xw_picked[:, lo:hi].bitcast(FP8X4),
+                rhs_scale=planes[:, H + lo : H + hi],
                 start=True,
                 stop=True,
             )
+            nc.scalar.copy(out=scores[t][:, lo:hi], in_=bank[:])
 
-        lead = [ps.tile([P, S // 2], F32, name="lead_bank%d" % h) for h in range(2)]
-        banks = [ps.tile([P, S], F32, name="score_bank%d" % t) for t in range(1, PACK)]
-        for h in range(2):
-            cols = slice(256 * h, 256 * (h + 1))
-            score_pass(lead[h][:], 0, h)
-            nc.scalar.copy(out=scores[0][:, cols], in_=lead[h][:])
-            for t in range(1, PACK):
-                score_pass(banks[t - 1][:, cols], t, h)
+        score(0, 0, 256)
+        score(0, 256, 512)
         for t in range(1, PACK):
-            nc.scalar.copy(out=scores[t][:], in_=banks[t - 1][:])
+            score(t, 0, S)
 
         first = tile("first", [P, PACK, V], F32)
         diff = tile("diff", [P, PACK, V], F32)
@@ -141,12 +138,12 @@ def tile_picked_scorepair_none_po_kernel(
             if lo == 0:
                 nc.scalar.activation(out=z32[:, t, :], in_=size[:, t, 0:HALF], func=ACT.Copy, scale=gn_t[:, t : t + 1])
 
-        z_codes = tile("z_codes", [P, V], U32)
+        z_codes = tile_at(G + 10 * T + 4 * S * 3, "z_codes", [P, V], U32)
         z_scales = tile("z_scales", [P, V], U8)
         y_codes = tile("y_codes", [P, V], U32)
         y_scales = tile("y_scales", [P, V], U8)
         z16 = [tile("z16_%d" % h, [P, HALF, PACK], BF16) for h in range(2)]
-        y16 = [tile("y16_%d" % h, [P, HALF, PACK], BF16) for h in range(2)]
+        y16 = tile("y16", [P, V, PACK], BF16)
         y32 = [tile("y32_%d" % h, [P, PACK, HALF], F32) for h in range(2)]
         out_rows = out_0.rearrange("(p t) v -> p t v", t=PACK)
         halves = [slice(0, HALF), slice(HALF, V)]
@@ -170,50 +167,48 @@ def tile_picked_scorepair_none_po_kernel(
         fetch_first(0, 0, V)
         fetch_second(0, 0, V)
         fetch_first(1, 0, V)
-        w1s = tile_at(G + 10 * T, "w1s", [P, N], U8)
-        nc.vector.tensor_copy(
-            out=w1s[:].rearrange("p (t m) -> p m t", t=PACK), in_=w1s_raw[:].rearrange("p (m t) -> p m t", t=PACK)
-        )
         fetch_first(2, 0, HALF)
         fetch_second(1, 0, V)
         fetch_first(3, 0, HALF)
         fetch_second(2, 0, HALF)
         fetch_second(3, 0, HALF)
-        nc.scalar.copy(out=z16[0][:], in_=z32[:].rearrange("p t v -> p v t"))
+        nc.scalar.copy(
+            out=z16[0][:].rearrange("p (c i) t -> p c t i", i=4), in_=z32[:].rearrange("p t (c i) -> p c t i", i=4)
+        )
         fetch_first(2, HALF, V)
         fetch_first(3, HALF, V)
         fetch_second(2, HALF, V)
         fetch_second(3, HALF, V)
 
+        w1s = tile_at(G + 10 * T + 4 * S * 3 + 4 * V, "w1s", [P, N], U8)
+        deal(w1s[:], w1s_raw[:], 16, 1)
         quantize(z_codes, z_scales, z16[0], 0)
         bank0 = ps.tile([P, PACK, HALF], F32, name="value_bank0")
         for t in range(PACK):
             value_pass(bank0[:, t, :], t, 0)
         nc.vector.tensor_tensor(
-            out=z16[1][:],
-            in0=size[:, :, halves[1]].rearrange("p t v -> p v t"),
-            in1=gn_t[:].unsqueeze(1).to_broadcast([P, HALF, PACK]),
+            out=z16[1][:].rearrange("p (c i) t -> p c t i", i=4),
+            in0=size[:, :, halves[1]].rearrange("p t (c i) -> p c t i", i=4),
+            in1=gn_t[:].unsqueeze(1).unsqueeze(3).to_broadcast([P, HALF // 4, PACK, 4]),
             op=ALU.mult,
         )
         quantize(z_codes, z_scales, z16[1], 1)
-        nc.scalar.copy(out=y16[0][:], in_=bank0[:].rearrange("p t v -> p v t"))
+        nc.scalar.copy(out=y16[:, halves[0], :], in_=bank0[:].rearrange("p t v -> p v t"))
         nc.scalar.copy(out=y32[0][:], in_=bank0[:])
         nc.sync.dma_start(out=out_rows[:, :, halves[0]], in_=y32[0][:])
-        quantize(y_codes, y_scales, y16[0], 0)
 
         for pair in range(2):
             rows = slice(2 * pair, 2 * pair + 2)
             bank = ps.tile([P, 2, HALF], F32, name="value_bank1_%d" % pair)
             for u in range(2):
                 value_pass(bank[:, u, :], 2 * pair + u, 1)
-            nc.vector.tensor_copy(out=y16[1][:, :, rows], in_=bank[:].rearrange("p t v -> p v t"))
+            nc.vector.tensor_copy(out=y16[:, halves[1], rows], in_=bank[:].rearrange("p t v -> p v t"))
             nc.scalar.copy(out=y32[1][:, rows, :], in_=bank[:])
-            queue = nc.sync if pair == 0 else nc.scalar
-            queue.dma_start(out=out_rows[:, rows, halves[1]], in_=y32[1][:, rows, :])
-        quantize(y_codes, y_scales, y16[1], 1)
+        nc.scalar.dma_start(out=out_rows[:, :, halves[1]], in_=y32[1][:])
+        nc.vector.quantize_mx(out=y_codes[:].bitcast(FP8X4), scales=y_scales[:], in_=y16[:].rearrange("p v t -> p (v t)"))
         nc.sync.dma_start(out=out_1[0].rearrange("p v r -> p (v r)").bitcast(I32), in_=y_codes[:].bitcast(I32))
         for q in range(4):
-            queue = nc.sync if q < 2 else nc.scalar
+            queue = nc.sync if q < 3 else nc.scalar
             queue.dma_start(
                 out=out_2[0, 4 * q : 4 * q + 4, :].bitcast(I32), in_=y_scales[32 * q : 32 * q + 4, :].bitcast(I32)
             )

@@ -69,7 +69,7 @@ def tile_picked_scorepair_none_po_kernel(
         nc.vector.tensor_copy(picked_bytes[:, 0:H], ds_win[:].indirect(kidx_t[:]))
         nc.vector.tensor_copy(picked_bytes[:, H : H + S], xs_win[:].indirect(offs_t[:]))
         for j in range(4):
-            nc.sync.dma_start(out=planes[j:P:32, :].bitcast(I32), in_=picked_bytes[8 * j : P : 32, :].bitcast(I32))
+            nc.scalar.dma_start(out=planes[j:P:32, :].bitcast(I32), in_=picked_bytes[8 * j : P : 32, :].bitcast(I32))
 
         dw_picked = tile_at(G + 9 * T, "dw_picked", [P, H], U32)
         nc.vector.tensor_copy(dw_picked[:], dw_win[:].indirect(kidx_t[:]))
@@ -165,8 +165,8 @@ def tile_picked_scorepair_none_po_kernel(
             )
 
         fetch_first(0, 0, V)
-        fetch_second(0, 0, V)
         fetch_first(1, 0, V)
+        fetch_second(0, 0, V)
         fetch_first(2, 0, HALF)
         fetch_second(1, 0, V)
         fetch_first(3, 0, HALF)
@@ -193,18 +193,26 @@ def tile_picked_scorepair_none_po_kernel(
             op=ALU.mult,
         )
         quantize(z_codes, z_scales, z16[1], 1)
-        nc.scalar.copy(out=y16[:, halves[0], :], in_=bank0[:].rearrange("p t v -> p v t"))
         nc.scalar.copy(out=y32[0][:], in_=bank0[:])
         nc.sync.dma_start(out=out_rows[:, :, halves[0]], in_=y32[0][:])
+        nc.vector.tensor_copy(out=y16[:, halves[0], :], in_=bank0[:].rearrange("p t v -> p v t"))
 
-        for pair in range(2):
-            rows = slice(2 * pair, 2 * pair + 2)
-            bank = ps.tile([P, 2, HALF], F32, name="value_bank1_%d" % pair)
-            for u in range(2):
-                value_pass(bank[:, u, :], 2 * pair + u, 1)
-            nc.vector.tensor_copy(out=y16[:, halves[1], rows], in_=bank[:].rearrange("p t v -> p v t"))
-            nc.scalar.copy(out=y32[1][:, rows, :], in_=bank[:])
-        nc.scalar.dma_start(out=out_rows[:, :, halves[1]], in_=y32[1][:])
+        pairs = [slice(0, 2), slice(2, 4)]
+        banks = [ps.tile([P, 2, HALF], F32, name="value_bank1_%d" % pair) for pair in range(2)]
+        for t in range(PACK):
+            value_pass(banks[t // 2][:, t % 2, :], t, 1)
+
+        def store_pair(pair, queue):
+            nc.scalar.copy(out=y32[1][:, pairs[pair], :], in_=banks[pair][:])
+            queue.dma_start(out=out_rows[:, pairs[pair], halves[1]], in_=y32[1][:, pairs[pair], :])
+
+        def round_pair(pair):
+            nc.vector.tensor_copy(out=y16[:, halves[1], pairs[pair]], in_=banks[pair][:].rearrange("p t v -> p v t"))
+
+        store_pair(0, nc.sync)
+        round_pair(1)
+        store_pair(1, nc.scalar)
+        round_pair(0)
         nc.vector.quantize_mx(out=y_codes[:].bitcast(FP8X4), scales=y_scales[:], in_=y16[:].rearrange("p v t -> p (v t)"))
         nc.sync.dma_start(out=out_1[0].rearrange("p v r -> p (v r)").bitcast(I32), in_=y_codes[:].bitcast(I32))
         for q in range(4):

from contextlib import ExitStack

import concourse.mybir as mybir

K, T, S, V, N, G, H = 512, 2048, 512, 256, 512, 2048, 512
FLOPS = 2 * K * H * S + 2 * H * N * V

F32 = mybir.dt.float32
BF16 = mybir.dt.bfloat16
I32 = mybir.dt.int32
U32 = mybir.dt.uint32
U16 = mybir.dt.uint16
U8 = mybir.dt.uint8
FP8X4 = mybir.dt.float8_e4m3fn_x4
FP4X4 = mybir.dt.float4_e2m1fn_x4
ACT = mybir.ActivationFunctionType
ALU = mybir.AluOpType

P = 128
PACK = 4
HALF = V // 2


def tile_picked_scorepair_none_po_kernel(
    tc, x_words, x_scales, d_words, d_scales, gn, w1_words, w1_scales, offs, kidx, l1, l2, out_0, out_1, out_2
):
    nc = tc.nc
    with ExitStack() as ctx:
        sb = ctx.enter_context(tc.tile_pool(name="sb", bufs=1))
        ps = ctx.enter_context(tc.psum_pool(name="ps", bufs=1))

        shared = ctx.enter_context(tc.tile_pool(name="shared", bufs=1))

        def tile(name, shape, dtype):
            return sb.tile(shape, dtype, name=name, align_bytes=64)

        def tile_at(offset, name, shape, dtype):
            return shared.tile(shape, dtype, name=name, align_bytes=64, offset=offset)

        kidx_t = tile("kidx_t", [P, H // 16], U16)
        offs_t = tile("offs_t", [P, S // 16], U16)
        l1_t = tile("l1_t", [P, V // 16], U16)
        l2_t = tile("l2_t", [P, V // 16], U16)
        ds_win = tile_at(0, "ds_win", [P, G], U8)
        xs_win = tile_at(G, "xs_win", [P, T], U8)
        dw_win = tile_at(G + 5 * T, "dw_win", [P, G], U32)
        xw_win = tile_at(G + T, "xw_win", [P, T], U32)
        warm_in = tile("warm_in", [P, 1], F32)
        warm_out = tile("warm_out", [P, 1], F32)

        nc.vector.memset(ds_win[:].bitcast(I32), 0)
        nc.vector.memset(xs_win[:].bitcast(I32), 0)

        nc.sync.dma_start(kidx_t[:], kidx)
        nc.sync.dma_start(offs_t[:], offs)
        nc.sync.dma_start(l1_t[:], l1)
        nc.sync.dma_start(l2_t[:], l2)
        nc.sync.dma_start(out=ds_win[0:P:8, :].bitcast(I32), in_=d_scales[0].bitcast(I32))
        nc.sync.dma_start(out=xs_win[0:P:8, :].bitcast(I32), in_=x_scales[0].bitcast(I32))
        nc.sync.dma_start(out=dw_win[:].bitcast(I32), in_=d_words[0].rearrange("p n t -> p (n t)").bitcast(I32))
        nc.sync.dma_start(out=xw_win[:].bitcast(I32), in_=x_words[0].rearrange("p n t -> p (n t)").bitcast(I32))

        planes = tile("planes", [P, H + S], U8)
        nc.vector.memset(planes[:].bitcast(I32), 0)
        nc.vector.memset(warm_in[:], 0.0)
        nc.scalar.activation(out=warm_out[:], in_=warm_in[:], func=ACT.Abs)

        picked_bytes = tile("picked_bytes", [P, H + S], U8)
        nc.vector.tensor_copy(picked_bytes[:, 0:H], ds_win[:].indirect(kidx_t[:]))
        nc.vector.tensor_copy(picked_bytes[:, H : H + S], xs_win[:].indirect(offs_t[:]))
        for j in range(4):
            nc.scalar.dma_start(out=planes[j:P:32, :].bitcast(I32), in_=picked_bytes[8 * j : P : 32, :].bitcast(I32))

        dw_picked = tile_at(G + 9 * T, "dw_picked", [P, H], U32)
        nc.vector.tensor_copy(dw_picked[:], dw_win[:].indirect(kidx_t[:]))
        gn_t = tile_at(G + 5 * T, "gn_t", [P, PACK], F32)
        w1w_raw = tile_at(G + 5 * T + N, "w1w_raw", [P, 2 * N], U8)
        nc.sync.dma_start(out=w1w_raw[:].bitcast(I32), in_=w1_words[0].bitcast(I32))
        nc.sync.dma_start(out=gn_t[:], in_=gn.rearrange("(p t) o -> p (t o)", t=PACK))

        def deal(dst, src, run, width):
            nc.vector.tensor_copy(
                out=dst.rearrange("p (t c i b) -> p c t i b", t=PACK, i=run, b=width),
                in_=src.rearrange("p (c i t b) -> p c t i b", t=PACK, i=run, b=width),
            )

        dw_dealt = tile("dw_dealt", [P, H], U32)
        deal(dw_dealt[:], dw_picked[:], 4, 1)
        xw_picked = tile_at(G + 9 * T, "xw_picked", [P, S], U32)
        nc.vector.tensor_copy(xw_picked[:, 0:256], xw_win[:].indirect(offs_t[:, 0:16]))
        ds_dealt = tile("ds_dealt", [P, H], U8)
        deal(ds_dealt[:], planes[:, 0:H], 16, 1)
        nc.vector.tensor_copy(xw_picked[:, 256:512], xw_win[:].indirect(offs_t[:, 16:32]))

        w1s_raw = tile_at(G + T + 2 * N, "w1s_raw", [P, N], U8)
        nc.vector.memset(w1s_raw[:].bitcast(I32), 0)
        for q in range(4):
            nc.sync.dma_start(
                out=w1s_raw[32 * q : 32 * q + 4, :].bitcast(I32), in_=w1_scales[0, 4 * q : 4 * q + 4, :].bitcast(I32)
            )

        w1w = tile_at(G + T, "w1w", [P, 2 * N], U8)
        deal(w1w[:], w1w_raw[:], 8, 2)

        scores = [tile_at(G + 10 * T + 4 * S * t, "scores%d" % t, [P, S], F32) for t in range(PACK)]

        def score(t, lo, hi):
            bank = ps.tile([P, hi - lo], F32, name="score_bank%d_%d" % (t, lo))
            nc.tensor.matmul_mx(
                out=bank[:],
                lhsT=dw_dealt[:, P * t : P * (t + 1)].bitcast(FP8X4),
                lhsT_scale=ds_dealt[:, P * t : P * (t + 1)],
                rhs=xw_picked[:, lo:hi].bitcast(FP8X4),
                rhs_scale=planes[:, H + lo : H + hi],
                start=True,
                stop=True,
            )
            nc.scalar.copy(out=scores[t][:, lo:hi], in_=bank[:])

        score(0, 0, 256)
        score(0, 256, 512)
        for t in range(1, PACK):
            score(t, 0, S)

        first = tile("first", [P, PACK, V], F32)
        diff = tile("diff", [P, PACK, V], F32)
        size = tile("size", [P, PACK, V], F32)
        z32 = tile("z32", [P, PACK, HALF], F32)

        def fetch_first(t, lo, hi):
            nc.vector.tensor_copy(first[:, t, lo:hi], scores[t][:].indirect(l1_t[:, lo // 16 : hi // 16]))

        def fetch_second(t, lo, hi):
            nc.vector.tensor_tensor(
                diff[:, t, lo:hi], scores[t][:].indirect(l2_t[:, lo // 16 : hi // 16]), first[:, t, lo:hi], ALU.subtract
            )
            nc.scalar.activation(out=size[:, t, lo:hi], in_=diff[:, t, lo:hi], func=ACT.Abs, scale=0.0625)
            if lo == 0:
                nc.scalar.activation(out=z32[:, t, :], in_=size[:, t, 0:HALF], func=ACT.Copy, scale=gn_t[:, t : t + 1])

        z_codes = tile_at(G + 10 * T + 4 * S * 3, "z_codes", [P, V], U32)
        z_scales = tile("z_scales", [P, V], U8)
        y_codes = tile("y_codes", [P, V], U32)
        y_scales = tile("y_scales", [P, V], U8)
        z16 = [tile("z16_%d" % h, [P, HALF, PACK], BF16) for h in range(2)]
        y16 = tile("y16", [P, V, PACK], BF16)
        y32 = [tile("y32_%d" % h, [P, PACK, HALF], F32) for h in range(2)]
        out_rows = out_0.rearrange("(p t) v -> p t v", t=PACK)
        halves = [slice(0, HALF), slice(HALF, V)]

        def quantize(codes, scales, src, h):
            nc.vector.quantize_mx(
                out=codes[:, halves[h]].bitcast(FP8X4), scales=scales[:, halves[h]], in_=src[:].rearrange("p v t -> p (v t)")
            )

        def value_pass(dst, t, h):
            nc.tensor.matmul_mx(
                out=dst,
                lhsT=w1w[:, 2 * P * t : 2 * P * (t + 1)].bitcast(FP4X4),
                lhsT_scale=w1s[:, P * t : P * (t + 1)],
                rhs=z_codes[:, halves[h]].bitcast(FP8X4),
                rhs_scale=z_scales[:, halves[h]],
                start=True,
                stop=True,
            )

        fetch_first(0, 0, V)
        fetch_first(1, 0, V)
        fetch_second(0, 0, V)
        fetch_first(2, 0, HALF)
        fetch_second(1, 0, V)
        fetch_first(3, 0, HALF)
        fetch_second(2, 0, HALF)
        fetch_second(3, 0, HALF)
        nc.scalar.copy(
            out=z16[0][:].rearrange("p (c i) t -> p c t i", i=4), in_=z32[:].rearrange("p t (c i) -> p c t i", i=4)
        )
        fetch_first(2, HALF, V)
        fetch_first(3, HALF, V)
        fetch_second(2, HALF, V)
        fetch_second(3, HALF, V)

        w1s = tile_at(G + 10 * T + 4 * S * 3 + 4 * V, "w1s", [P, N], U8)
        deal(w1s[:], w1s_raw[:], 16, 1)
        quantize(z_codes, z_scales, z16[0], 0)
        bank0 = ps.tile([P, PACK, HALF], F32, name="value_bank0")
        for t in range(PACK):
            value_pass(bank0[:, t, :], t, 0)
        nc.vector.tensor_tensor(
            out=z16[1][:].rearrange("p (c i) t -> p c t i", i=4),
            in0=size[:, :, halves[1]].rearrange("p t (c i) -> p c t i", i=4),
            in1=gn_t[:].unsqueeze(1).unsqueeze(3).to_broadcast([P, HALF // 4, PACK, 4]),
            op=ALU.mult,
        )
        quantize(z_codes, z_scales, z16[1], 1)
        nc.scalar.copy(out=y32[0][:], in_=bank0[:])
        nc.sync.dma_start(out=out_rows[:, :, halves[0]], in_=y32[0][:])
        nc.vector.tensor_copy(out=y16[:, halves[0], :], in_=bank0[:].rearrange("p t v -> p v t"))

        pairs = [slice(0, 2), slice(2, 4)]
        banks = [ps.tile([P, 2, HALF], F32, name="value_bank1_%d" % pair) for pair in range(2)]
        for t in range(PACK):
            value_pass(banks[t // 2][:, t % 2, :], t, 1)

        def store_pair(pair, queue):
            nc.scalar.copy(out=y32[1][:, pairs[pair], :], in_=banks[pair][:])
            queue.dma_start(out=out_rows[:, pairs[pair], halves[1]], in_=y32[1][:, pairs[pair], :])

        def round_pair(pair):
            nc.vector.tensor_copy(out=y16[:, halves[1], pairs[pair]], in_=banks[pair][:].rearrange("p t v -> p v t"))

        store_pair(0, nc.sync)
        round_pair(1)
        store_pair(1, nc.scalar)
        round_pair(0)
        nc.vector.quantize_mx(out=y_codes[:].bitcast(FP8X4), scales=y_scales[:], in_=y16[:].rearrange("p v t -> p (v t)"))
        nc.sync.dma_start(out=out_1[0].rearrange("p v r -> p (v r)").bitcast(I32), in_=y_codes[:].bitcast(I32))
        for q in range(4):
            queue = nc.sync if q < 3 else nc.scalar
            queue.dma_start(
                out=out_2[0, 4 * q : 4 * q + 4, :].bitcast(I32), in_=y_scales[32 * q : 32 * q + 4, :].bitcast(I32)
            )
